import numpy as np
import ml_dtypes


def mxq(x, axis, fmt="e4m3"):
    dtype, down = {"e4m3": (ml_dtypes.float8_e4m3fn, 7), "e5m2": (ml_dtypes.float8_e5m2, 14)}[fmt]
    v = np.moveaxis(np.asarray(x, np.float32).astype(ml_dtypes.bfloat16).astype(np.float64), axis, -1)
    blocks = v.reshape(v.shape[:-1] + (-1, 32))
    amax = np.abs(blocks).max(-1, keepdims=True)
    byte = np.maximum(np.where(amax > 0, np.frexp(amax)[1] - 1 + 127, 0) - down, 1)
    scale = np.exp2(byte - 127.0)
    codes = (blocks / scale).astype(np.float32).astype(dtype).astype(np.float64)
    return np.moveaxis((codes * scale).reshape(v.shape), -1, axis)


WIDE = False


def mx_kscale(k):
    if not WIDE:
        return np.ones(k)
    levels = np.array([10, -10, 5, -5, 0])
    if k % 512:
        return np.exp2(np.random.permutation(np.resize(levels, k // 32))).repeat(32)
    a = np.empty((k // 512, 16))
    for p in range(k // 512):
        a[p, :8] = np.random.permutation(np.resize(levels, 8))
        for g in range(8):
            far = levels[np.abs(levels - a[p, g]) >= 10]
            a[p, g + 8] = far[np.random.randint(len(far))]
    return np.exp2(a.ravel()).repeat(32)


def f64(x):
    return np.asarray(x).astype(np.float64)


def striped(idx):
    return np.tile(np.asarray(idx).reshape(-1, 16).T, (8, 1)).astype(np.uint16)


def unstriped(offs):
    return offs[:16].T.reshape(-1).astype(np.int64)


E2M1 = np.array([0.0, 0.5, 1.0, 1.5, 2.0, 3.0, 4.0, 6.0, -0.0, -0.5, -1.0, -1.5, -2.0, -3.0, -4.0, -6.0])


def pack_weight(w, fmt):
    k, n = w.shape
    w = f64(np.asarray(w, np.float32).astype(ml_dtypes.bfloat16)).reshape(k // 32, 32, n)
    amax = np.abs(w).max(1)
    if fmt == "e4m3":
        byte = np.frexp(amax)[1] - 1 + 127 - 7
    else:
        mant, ex = np.frexp(amax / 6.0)
        byte = np.where(mant > 0.5, ex, ex - 1) + 127
    byte = np.clip(np.where(amax > 0, byte, 1), 1, 254)
    scaled = (w * np.exp2(127.0 - byte)[:, None, :]).reshape(k, n).astype(np.float32)
    by_word = np.ascontiguousarray(scaled.reshape(k // 512, 128, 4, n).transpose(0, 1, 3, 2))
    if fmt == "e4m3":
        words = by_word.astype(ml_dtypes.float8_e4m3fn).view(np.uint8)
    else:
        c = by_word.astype(ml_dtypes.float4_e2m1fn).view(np.uint8) & 0xF
        words = (c[..., 0::2] | (c[..., 1::2] << 4)).reshape(k // 512, 128, 2 * n)
    return np.ascontiguousarray(words), np.ascontiguousarray(byte.astype(np.uint8).reshape(k // 512, 16, n))


def unpack_weight(words, scales, fmt):
    g, _, n = scales.shape
    words = np.ascontiguousarray(words).reshape(g, 128, n, -1)
    if fmt == "e4m3":
        vals = words.view(ml_dtypes.float8_e4m3fn).astype(np.float64)
    else:
        nib = np.empty((g, 128, n, 4), np.uint8)
        nib[..., 0::2] = words & 0xF
        nib[..., 1::2] = words >> 4
        vals = E2M1[nib]
    vals = vals * np.repeat(np.exp2(scales.astype(np.float64) - 127.0), 8, axis=1)[..., None]
    return vals.transpose(0, 1, 3, 2).reshape(g * 512, n)


D, T, I, J, U, E, Y = 512, 2048, 512, 512, 1024, 512, 1024


def setup_inputs():
    n = np.random.standard_normal
    idx = np.random.permutation(T)[:I]
    idx2 = np.random.permutation(U)[:J]
    idx3 = np.random.permutation(U)[:J]
    idx4 = np.random.permutation(Y)[:I]
    fd = mx_kscale(D)
    fi = mx_kscale(I)
    ti = np.ones(T)
    ti[idx] = fi
    ti4 = np.ones(Y)
    ti4[idx4] = fi
    keysp = pack_weight(n((D, T)) / fd[:, None], "e4m3")
    return {
        "keys_words": keysp[0],
        "keys_scales": keysp[1],
        "notes": (n((D, U)) * 1.0 / np.sqrt(D) * fd[:, None]).astype(np.float32),
        "rowf": (np.random.uniform(0.02, 0.08, (I, 1)) * fi[:, None]).astype(np.float32),
        "rowf2": (np.random.uniform(0.02, 0.08, (I, 1)) * fi[:, None]).astype(np.float32),
        "vals": (n((E, T)) / ti).astype(np.float32),
        "vals2": (n((E, Y)) / ti4).astype(np.float32),
        "offs": striped(idx),
        "offs2": striped(idx2),
        "offs3": striped(idx3),
        "offs4": striped(idx4),
    }


def reference(keys_words, keys_scales, notes, rowf, rowf2, vals, vals2, offs, offs2, offs3, offs4):
    idx = unstriped(offs)
    idx2 = unstriped(offs2)
    idx3 = unstriped(offs3)
    idx4 = unstriped(offs4)
    keysu = unpack_weight(keys_words, keys_scales, "e4m3")
    keysidxg = keysu[:, idx]
    notesq = mxq(f64(notes), 0, "e4m3")
    g1 = keysidxg.T @ notesq
    g9 = g1[:, idx2] - g1[:, idx3]
    g0 = np.maximum(g9, 0.0)
    gr1 = g0 * f64(rowf)
    gr2 = g0 * f64(rowf2)
    vt1 = f64(vals)[:, idx].T
    vt2 = f64(vals2)[:, idx4].T
    vt1q = mxq(vt1, 0, "e4m3")
    gr1q = mxq(gr1, 0, "e4m3")
    vt2q = mxq(vt2, 0, "e4m3")
    gr2q = mxq(gr2, 0, "e4m3")
    o = vt1q.T @ gr1q + vt2q.T @ gr2q
    return o

@@ -1,0 +1,199 @@
+from contextlib import ExitStack
+
+import concourse.mybir as mybir
+from concourse.masks import make_identity
+
+F32 = mybir.dt.float32
+BF16 = mybir.dt.bfloat16
+I32 = mybir.dt.int32
+U32 = mybir.dt.uint32
+U16 = mybir.dt.uint16
+U8 = mybir.dt.uint8
+FP8X4 = mybir.dt.float8_e4m3fn_x4
+ALU = mybir.AluOpType
+COPY = mybir.ActivationFunctionType.Copy
+
+P = 128
+PACK = 4
+D, T, I, J, U, E, Y = 512, 2048, 512, 512, 1024, 512, 1024
+HALF = U // 2
+FLOPS = 2 * D * I * U + 2 * 2 * I * E * J
+
+
+def woven(dst, src):
+    return (
+        dst.rearrange("p (c i) t -> p c t i", i=4),
+        src.rearrange("p t (c i) -> p c t i", i=4),
+    )
+
+
+def tile_attend_tab_looked_twostores_kernel(
+    tc, keys_words, keys_scales, notes, rowf, rowf2, vals, vals2, offs, offs2, offs3, offs4, out
+):
+    nc = tc.nc
+    with ExitStack() as ctx:
+        keep = ctx.enter_context(tc.tile_pool(name="keep", bufs=1))
+        psum = ctx.enter_context(tc.psum_pool(name="psum", bufs=1))
+
+        def sb(name, shape, dtype):
+            return keep.tile(shape, dtype, name=name, align_bytes=64)
+
+        lists = {n: sb(n, [P, 32], U16) for n in ("offs", "offs2", "offs3", "offs4")}
+        pool_words = sb("pool_words", [P, T], U32)
+        pool_scales = sb("pool_scales", [P, T], U8)
+        note_cols = [(0, 512), (512, 768), (768, 1024)]
+        note_raw = [sb("note_raw%d" % n, [P, PACK, b - a], F32) for n, (a, b) in enumerate(note_cols)]
+        factors = [sb("factor%d" % s, [P, PACK], F32) for s in range(2)]
+        stores = [
+            [sb("store0_%d" % b, [P, T], F32) for b in range(3)]
+            + [keep.tile([P, T], F32, name="store0_3", tag="last_store", align_bytes=64)],
+            [sb("store1_%d" % b, [P, Y], F32) for b in range(4)],
+        ]
+        notes_by_row = notes.rearrange("(p t) u -> p t u", t=PACK)
+
+        nc.gpsimd.memset(pool_scales[:].bitcast(I32), 0)
+        for name, src in (("offs", offs), ("offs3", offs3), ("offs2", offs2), ("offs4", offs4)):
+            nc.sync.dma_start(lists[name][:], src)
+        nc.sync.dma_start(out=note_raw[0][:], in_=notes_by_row[:, :, 0:512])
+        for q in range(4):
+            nc.sync.dma_start(
+                out=pool_scales[32 * q : 32 * q + 4, :].bitcast(I32),
+                in_=keys_scales[0, 4 * q : 4 * q + 4, :].bitcast(I32),
+            )
+        nc.sync.dma_start(
+            out=pool_words[:].bitcast(I32),
+            in_=keys_words[0].rearrange("p n t -> p (n t)").bitcast(I32),
+        )
+        for n in (1, 2):
+            a, b = note_cols[n]
+            nc.sync.dma_start(out=note_raw[n][:], in_=notes_by_row[:, :, a:b])
+        for s, src in enumerate((rowf, rowf2)):
+            nc.sync.dma_start(out=factors[s][:], in_=src.rearrange("(p t) o -> p (t o)", t=PACK))
+        for s in (1, 0):
+            for b in range(4):
+                nc.sync.dma_start(out=stores[s][b][:], in_=(vals, vals2)[s][b * P : (b + 1) * P, :])
+
+        ident = sb("ident", [P, P], F32)
+        make_identity(nc, ident[:])
+
+        key_scales = sb("key_scales", [P, I], U8)
+        key_words = sb("key_words", [P, I], U32)
+        nc.vector.tensor_copy(
+            key_scales[:].rearrange("p (r s) -> p s r", r=PACK),
+            pool_scales[:].indirect(lists["offs"][:]),
+        )
+
+        note_bf = [sb("note_bf%d" % h, [P, HALF, PACK], BF16) for h in range(2)]
+        note_codes = [sb("note_codes%d" % h, [P, HALF], U32) for h in range(2)]
+        note_scales = [sb("note_scales%d" % h, [P, HALF], U8) for h in range(2)]
+
+        def quantize(codes, scales, grouped):
+            nc.vector.quantize_mx(
+                out=codes.bitcast(FP8X4), scales=scales, in_=grouped.rearrange("p w t -> p (w t)")
+            )
+
+        dst, src = woven(note_bf[0][:, 0:320, :], note_raw[0][:, :, 0:320])
+        nc.vector.tensor_copy(dst, src)
+        dst, src = woven(note_bf[0][:, 320:512, :], note_raw[0][:, :, 320:512])
+        nc.scalar.activation(dst, src, COPY)
+        quantize(note_codes[0][:], note_scales[0][:], note_bf[0][:])
+        nc.vector.tensor_copy(
+            key_words[:].rearrange("p (r s) -> p s r", r=PACK),
+            pool_words[:].indirect(lists["offs"][:]),
+        )
+        for n in (1, 2):
+            cols = slice((n - 1) * 256, n * 256)
+            dst, src = woven(note_bf[1][:, cols, :], note_raw[n][:])
+            nc.vector.tensor_copy(dst, src)
+        for n in (1, 2):
+            cols = slice((n - 1) * 256, n * 256)
+            quantize(note_codes[1][:, cols], note_scales[1][:, cols], note_bf[1][:, cols, :])
+
+        wide = [sb("wide%d" % r, [P, U], F32) for r in range(PACK)]
+        for h in range(2):
+            for r in range(PACK):
+                bank = psum.tile([P, HALF], F32, name="wide_bank", tag="wide_bank", bufs=4)
+                rows = slice(r * P, (r + 1) * P)
+                nc.tensor.matmul_mx(
+                    out=bank[:],
+                    lhsT=key_words[:, rows].bitcast(FP8X4),
+                    lhsT_scale=key_scales[:, rows],
+                    rhs=note_codes[h][:].bitcast(FP8X4),
+                    rhs_scale=note_scales[h][:],
+                    start=True,
+                    stop=True,
+                )
+                nc.scalar.copy(wide[r][:, h * HALF : (h + 1) * HALF], bank[:])
+
+        planes = [sb("planes%d" % s, [P, PACK, J], BF16) for s in range(2)]
+        for r in range(PACK):
+            minus = sb("minus%d" % r, [P, J], F32)
+            diff = sb("diff%d" % r, [P, J], F32)
+            nc.scalar.activation(minus[:], wide[r][:].indirect(lists["offs3"][:]), COPY)
+            nc.vector.tensor_tensor(diff[:], wide[r][:].indirect(lists["offs2"][:]), minus[:], ALU.subtract)
+            for s in (1, 0):
+                nc.vector.tensor_scalar(
+                    planes[s][:, r, :], diff[:], 0.0, factors[s][:, r : r + 1], ALU.max, ALU.mult
+                )
+        table_bf = [sb("table_bf%d" % s, [P, J, PACK], BF16) for s in range(2)]
+        table_codes = [
+            None,
+            sb("table_codes1", [P, J], U32),
+        ]
+        table_scales = [sb("table_scales%d" % s, [P, J], U8) for s in range(2)]
+        for s in (1, 0):
+            dst, src = woven(table_bf[s][:], planes[s][:])
+            nc.vector.tensor_copy(dst, src)
+        quantize(table_codes[1][:], table_scales[1][:], table_bf[1][:])
+
+        store_lists = (lists["offs"], lists["offs4"])
+        val_codes = [sb("val_codes%d" % s, [P, E], U32) for s in range(2)]
+        val_scales = [sb("val_scales%d" % s, [P, E], U8) for s in range(2)]
+        val_bf = {}
+        for s, blocks, leave in (
+            (1, (0, 1), nc.vector.tensor_copy),
+            (1, (2, 3), nc.scalar.copy),
+            (0, (0, 1), nc.vector.tensor_copy),
+            (0, (2, 3), nc.vector.tensor_copy),
+        ):
+            n = len(blocks)
+            turned = psum.tile([P, n, 2, P], F32, name="turned", tag="turned", bufs=4)
+            for place, b in enumerate(blocks):
+                picked = sb("picked%d_%d" % (s, b), [P, I], BF16)
+                window = stores[s][b][:].indirect(store_lists[s][:])
+                if b == 0 and s == 1:
+                    nc.vector.tensor_copy(picked[:], window)
+                else:
+                    nc.scalar.activation(picked[:], window, COPY)
+                words = picked[:].bitcast(F32)
+                for u in range(2):
+                    nc.tensor.transpose(turned[:, place, u, :], words[:, u : 2 * P : 2], ident[:])
+            if (s, blocks) == (0, (2, 3)):
+                table_codes[0] = keep.tile([P, J], U32, name="table_codes0", tag="last_store", align_bytes=64)
+                quantize(table_codes[0][:], table_scales[0][:], table_bf[0][:])
+            grouped = sb("val_bf%d_%d" % (s, blocks[0]), [P, n * P, PACK], BF16)
+            val_bf[s, blocks[0]] = grouped
+            leave(
+                grouped[:].rearrange("p w t -> p (w t)").bitcast(F32).rearrange("p (n e u) -> p n e u", n=n, u=2),
+                turned[:].rearrange("p n u e -> p n e u"),
+            )
+            cols = slice(blocks[0] * P, (blocks[0] + n) * P)
+            quantize(val_codes[s][:, cols], val_scales[s][:, cols], grouped[:])
+
+        accs = [psum.tile([P, J], F32, name="acc%d" % b, tag="wide_bank", bufs=4) for b in range(4)]
+        for s in (1, 0):
+            for b in range(4):
+                cols = slice(b * P, (b + 1) * P)
+                nc.tensor.matmul_mx(
+                    out=accs[b][:],
+                    lhsT=val_codes[s][:, cols].bitcast(FP8X4),
+                    lhsT_scale=val_scales[s][:, cols],
+                    rhs=table_codes[s][:].bitcast(FP8X4),
+                    rhs_scale=table_scales[s][:],
+                    start=(s == 1),
+                    stop=(s == 0),
+                )
+        for b in range(4):
+            result = sb("result%d" % b, [P, J], F32)
+            (nc.scalar.copy if b % 2 == 0 else nc.vector.tensor_copy)(result[:], accs[b][:])
+            nc.sync.dma_start(out=out[b * P : (b + 1) * P, :], in_=result[:])

@@ -45,15 +45,16 @@ def tile_attend_tab_looked_twostores_kernel(
         note_raw = [sb("note_raw%d" % n, [P, PACK, b - a], F32) for n, (a, b) in enumerate(note_cols)]
         factors = [sb("factor%d" % s, [P, PACK], F32) for s in range(2)]
         stores = [
-            [sb("store0_%d" % b, [P, T], F32) for b in range(3)]
-            + [keep.tile([P, T], F32, name="store0_3", tag="last_store", align_bytes=64)],
+            [sb("store0_%d" % b, [P, T], F32) for b in range(4)],
             [sb("store1_%d" % b, [P, Y], F32) for b in range(4)],
         ]
         notes_by_row = notes.rearrange("(p t) u -> p t u", t=PACK)
 
         nc.gpsimd.memset(pool_scales[:].bitcast(I32), 0)
-        for name, src in (("offs", offs), ("offs3", offs3), ("offs2", offs2), ("offs4", offs4)):
-            nc.sync.dma_start(lists[name][:], src)
+        nc.sync.dma_start(lists["offs"][:], offs)
+        nc.sync.dma_start(lists["offs3"][:], offs3)
+        nc.sync.dma_start(lists["offs2"][:], offs2)
+        nc.sync.dma_start(lists["offs4"][:], offs4)
         nc.sync.dma_start(out=note_raw[0][:], in_=notes_by_row[:, :, 0:512])
         for q in range(4):
             nc.sync.dma_start(
@@ -83,7 +84,10 @@ def tile_attend_tab_looked_twostores_kernel(
             pool_scales[:].indirect(lists["offs"][:]),
         )
 
-        note_bf = [sb("note_bf%d" % h, [P, HALF, PACK], BF16) for h in range(2)]
+        note_bf = [
+            keep.tile([P, HALF, PACK], BF16, name="note_bf%d" % h, tag="note_bf%d" % h, align_bytes=64)
+            for h in range(2)
+        ]
         note_codes = [sb("note_codes%d" % h, [P, HALF], U32) for h in range(2)]
         note_scales = [sb("note_scales%d" % h, [P, HALF], U8) for h in range(2)]
 
@@ -109,7 +113,12 @@ def tile_attend_tab_looked_twostores_kernel(
             cols = slice((n - 1) * 256, n * 256)
             quantize(note_codes[1][:, cols], note_scales[1][:, cols], note_bf[1][:, cols, :])
 
-        wide = [sb("wide%d" % r, [P, U], F32) for r in range(PACK)]
+        first = keep.tile([P, I], BF16, name="picked1_0", tag="note_bf1", align_bytes=64)
+        nc.vector.tensor_copy(first[:], stores[1][0][:].indirect(lists["offs4"][:]))
+
+        wide = [
+            keep.tile([P, U], F32, name="wide%d" % r, tag="wide%d" % r, align_bytes=64) for r in range(PACK)
+        ]
         for h in range(2):
             for r in range(PACK):
                 bank = psum.tile([P, HALF], F32, name="wide_bank", tag="wide_bank", bufs=4)
@@ -123,65 +132,74 @@ def tile_attend_tab_looked_twostores_kernel(
                     start=True,
                     stop=True,
                 )
-                nc.scalar.copy(wide[r][:, h * HALF : (h + 1) * HALF], bank[:])
+                (nc.vector.tensor_copy if h == 1 and r > 0 else nc.scalar.copy)(wide[r][:, h * HALF : (h + 1) * HALF], bank[:])
 
-        planes = [sb("planes%d" % s, [P, PACK, J], BF16) for s in range(2)]
+        planes = [
+            keep.tile([P, PACK, J], BF16, name="planes%d" % s, tag="planes%d" % s, align_bytes=64) for s in range(2)
+        ]
         for r in range(PACK):
-            minus = sb("minus%d" % r, [P, J], F32)
-            diff = sb("diff%d" % r, [P, J], F32)
+            minus = keep.tile([P, J], F32, name="minus%d" % r, tag="minus%d" % r, align_bytes=64)
+            diff = keep.tile([P, J], F32, name="diff%d" % r, tag="diff%d" % r, align_bytes=64)
             nc.scalar.activation(minus[:], wide[r][:].indirect(lists["offs3"][:]), COPY)
             nc.vector.tensor_tensor(diff[:], wide[r][:].indirect(lists["offs2"][:]), minus[:], ALU.subtract)
             for s in (1, 0):
                 nc.vector.tensor_scalar(
                     planes[s][:, r, :], diff[:], 0.0, factors[s][:, r : r + 1], ALU.max, ALU.mult
                 )
-        table_bf = [sb("table_bf%d" % s, [P, J, PACK], BF16) for s in range(2)]
+        table_bf = [None, sb("table_bf1", [P, J, PACK], BF16)]
         table_codes = [
             None,
             sb("table_codes1", [P, J], U32),
         ]
         table_scales = [sb("table_scales%d" % s, [P, J], U8) for s in range(2)]
-        for s in (1, 0):
-            dst, src = woven(table_bf[s][:], planes[s][:])
-            nc.vector.tensor_copy(dst, src)
+        dst, src = woven(table_bf[1][:], planes[1][:])
+        nc.vector.tensor_copy(dst, src)
         quantize(table_codes[1][:], table_scales[1][:], table_bf[1][:])
 
         store_lists = (lists["offs"], lists["offs4"])
-        val_codes = [sb("val_codes%d" % s, [P, E], U32) for s in range(2)]
-        val_scales = [sb("val_scales%d" % s, [P, E], U8) for s in range(2)]
-        val_bf = {}
-        for s, blocks, leave in (
-            (1, (0, 1), nc.vector.tensor_copy),
-            (1, (2, 3), nc.scalar.copy),
-            (0, (0, 1), nc.vector.tensor_copy),
-            (0, (2, 3), nc.vector.tensor_copy),
-        ):
-            n = len(blocks)
-            turned = psum.tile([P, n, 2, P], F32, name="turned", tag="turned", bufs=4)
+
+        after = {(1, 1): "wide0", (1, 2): "wide1", (1, 3): "wide2", (0, 0): "wide3"}
+
+        def turn(s, blocks):
+            turned = psum.tile([P, 2, 2, P], F32, name="turned", tag="turned", bufs=4)
             for place, b in enumerate(blocks):
-                picked = sb("picked%d_%d" % (s, b), [P, I], BF16)
-                window = stores[s][b][:].indirect(store_lists[s][:])
                 if b == 0 and s == 1:
-                    nc.vector.tensor_copy(picked[:], window)
+                    picked = first
                 else:
-                    nc.scalar.activation(picked[:], window, COPY)
+                    name = "picked%d_%d" % (s, b)
+                    picked = keep.tile([P, I], BF16, name=name, tag=after.get((s, b), name), align_bytes=64)
+                    window = stores[s][b][:]
+                    if (s, b) == (0, 1):
+                        nc.scalar.activation(picked[:, 0:256], window.indirect(store_lists[s][:, 0:16]), COPY)
+                        nc.vector.tensor_copy(picked[:, 256:512], window.indirect(store_lists[s][:, 16:32]))
+                    else:
+                        nc.scalar.activation(picked[:], window.indirect(store_lists[s][:]), COPY)
                 words = picked[:].bitcast(F32)
                 for u in range(2):
                     nc.tensor.transpose(turned[:, place, u, :], words[:, u : 2 * P : 2], ident[:])
-            if (s, blocks) == (0, (2, 3)):
-                table_codes[0] = keep.tile([P, J], U32, name="table_codes0", tag="last_store", align_bytes=64)
-                quantize(table_codes[0][:], table_scales[0][:], table_bf[0][:])
-            grouped = sb("val_bf%d_%d" % (s, blocks[0]), [P, n * P, PACK], BF16)
-            val_bf[s, blocks[0]] = grouped
+            return turned
+
+        def weave(leave, grouped, turned):
             leave(
-                grouped[:].rearrange("p w t -> p (w t)").bitcast(F32).rearrange("p (n e u) -> p n e u", n=n, u=2),
+                grouped.rearrange("p w t -> p (w t)").bitcast(F32).rearrange("p (n e u) -> p n e u", n=2, u=2),
                 turned[:].rearrange("p n u e -> p n e u"),
             )
-            cols = slice(blocks[0] * P, (blocks[0] + n) * P)
-            quantize(val_codes[s][:, cols], val_scales[s][:, cols], grouped[:])
 
+        val_scales = [sb("val_scales%d" % s, [P, E], U8) for s in range(2)]
+        val_codes = [
+            sb("val_codes0", [P, E], U32),
+            keep.tile([P, E], U32, name="val_codes1", tag="planes1", align_bytes=64),
+        ]
+        val_bf1 = keep.tile([P, E, PACK], BF16, name="val_bf1", tag="val_bf1", align_bytes=64)
+        weave(nc.scalar.copy, val_bf1[:, 0:256, :], turn(1, (0, 1)))
+        weave(nc.scalar.copy, val_bf1[:, 256:512, :], turn(1, (2, 3)))
+        quantize(val_codes[1][:], val_scales[1][:], val_bf1[:])
+        table_bf[0] = keep.tile([P, J, PACK], BF16, name="table_bf0", tag="val_bf1", align_bytes=64)
+        dst, src = woven(table_bf[0][:], planes[0][:])
+        nc.vector.tensor_copy(dst, src)
         accs = [psum.tile([P, J], F32, name="acc%d" % b, tag="wide_bank", bufs=4) for b in range(4)]
-        for s in (1, 0):
+
+        def product(s):
             for b in range(4):
                 cols = slice(b * P, (b + 1) * P)
                 nc.tensor.matmul_mx(
@@ -193,6 +211,20 @@ def tile_attend_tab_looked_twostores_kernel(
                     start=(s == 1),
                     stop=(s == 0),
                 )
+
+        low = turn(0, (0, 1))
+        product(1)
+        high = turn(0, (2, 3))
+        val_bf0a = sb("val_bf0a", [P, 256, PACK], BF16)
+        val_bf0b = sb("val_bf0b", [P, 256, PACK], BF16)
+        weave(nc.scalar.copy, val_bf0a[:], low)
+        weave(nc.scalar.copy, val_bf0b[:], high)
+        table_codes[0] = sb("table_codes0", [P, J], U32)
+        quantize(table_codes[0][:], table_scales[0][:], table_bf[0][:])
+        quantize(val_codes[0][:, 0:256], val_scales[0][:, 0:256], val_bf0a[:])
+        quantize(val_codes[0][:, 256:512], val_scales[0][:, 256:512], val_bf0b[:])
+
+        product(0)
         for b in range(4):
             result = sb("result%d" % b, [P, J], F32)
             (nc.scalar.copy if b % 2 == 0 else nc.vector.tensor_copy)(result[:], accs[b][:])

@@ -45,7 +45,8 @@ def tile_attend_tab_looked_twostores_kernel(
         note_raw = [sb("note_raw%d" % n, [P, PACK, b - a], F32) for n, (a, b) in enumerate(note_cols)]
         factors = [sb("factor%d" % s, [P, PACK], F32) for s in range(2)]
         stores = [
-            [sb("store0_%d" % b, [P, T], F32) for b in range(4)],
+            [sb("store0_%d" % b, [P, T], F32) for b in range(3)]
+            + [keep.tile([P, T], F32, name="store0_3", tag="last_store", align_bytes=64)],
             [sb("store1_%d" % b, [P, Y], F32) for b in range(4)],
         ]
         notes_by_row = notes.rearrange("(p t) u -> p t u", t=PACK)
@@ -68,11 +69,12 @@ def tile_attend_tab_looked_twostores_kernel(
         for n in (1, 2):
             a, b = note_cols[n]
             nc.sync.dma_start(out=note_raw[n][:], in_=notes_by_row[:, :, a:b])
+        for b in range(4):
+            nc.sync.dma_start(out=stores[1][b][:], in_=vals2[b * P : (b + 1) * P, :])
         for s, src in enumerate((rowf, rowf2)):
             nc.sync.dma_start(out=factors[s][:], in_=src.rearrange("(p t) o -> p (t o)", t=PACK))
-        for s in (1, 0):
-            for b in range(4):
-                nc.sync.dma_start(out=stores[s][b][:], in_=(vals, vals2)[s][b * P : (b + 1) * P, :])
+        for b in range(4):
+            nc.sync.dma_start(out=stores[0][b][:], in_=vals[b * P : (b + 1) * P, :])
 
         ident = sb("ident", [P, P], F32)
         make_identity(nc, ident[:])
@@ -134,53 +136,45 @@ def tile_attend_tab_looked_twostores_kernel(
                 )
                 (nc.vector.tensor_copy if h == 1 and r > 0 else nc.scalar.copy)(wide[r][:, h * HALF : (h + 1) * HALF], bank[:])
 
-        planes = [
-            keep.tile([P, PACK, J], BF16, name="planes%d" % s, tag="planes%d" % s, align_bytes=64) for s in range(2)
-        ]
+        second = sb("picked1_1", [P, I], BF16)
+        nc.vector.tensor_copy(second[:], stores[1][1][:].indirect(lists["offs4"][:]))
+        picked = {(1, 0): first, (1, 1): second}
+
+        def scale_rows(planes, s, r):
+            nc.vector.tensor_scalar(planes[:, r, :], diffs[r][:], 0.0, factors[s][:, r : r + 1], ALU.max, ALU.mult)
+
+        planes1 = keep.tile([P, PACK, J], BF16, name="planes1", tag="planes1", align_bytes=64)
+        diffs = []
         for r in range(PACK):
-            minus = keep.tile([P, J], F32, name="minus%d" % r, tag="minus%d" % r, align_bytes=64)
-            diff = keep.tile([P, J], F32, name="diff%d" % r, tag="diff%d" % r, align_bytes=64)
+            minus = sb("minus%d" % r, [P, J], F32)
+            diffs.append(sb("diff%d" % r, [P, J], F32))
             nc.scalar.activation(minus[:], wide[r][:].indirect(lists["offs3"][:]), COPY)
-            nc.vector.tensor_tensor(diff[:], wide[r][:].indirect(lists["offs2"][:]), minus[:], ALU.subtract)
-            for s in (1, 0):
-                nc.vector.tensor_scalar(
-                    planes[s][:, r, :], diff[:], 0.0, factors[s][:, r : r + 1], ALU.max, ALU.mult
-                )
-        table_bf = [None, sb("table_bf1", [P, J, PACK], BF16)]
-        table_codes = [
-            None,
-            sb("table_codes1", [P, J], U32),
-        ]
+            nc.vector.tensor_tensor(diffs[r][:], wide[r][:].indirect(lists["offs2"][:]), minus[:], ALU.subtract)
+            scale_rows(planes1, 1, r)
+
+        table_bf = [sb("table_bf%d" % s, [P, J, PACK], BF16) for s in range(2)]
+        table_codes = [sb("table_codes%d" % s, [P, J], U32) for s in range(2)]
         table_scales = [sb("table_scales%d" % s, [P, J], U8) for s in range(2)]
-        dst, src = woven(table_bf[1][:], planes[1][:])
-        nc.vector.tensor_copy(dst, src)
+        nc.vector.tensor_copy(*woven(table_bf[1][:], planes1[:]))
         quantize(table_codes[1][:], table_scales[1][:], table_bf[1][:])
 
         store_lists = (lists["offs"], lists["offs4"])
-
-        after = {(1, 1): "wide0", (1, 2): "wide1", (1, 3): "wide2", (0, 0): "wide3"}
+        after = {(1, 2): "wide0", (1, 3): "wide1", (0, 0): "wide2"}
 
         def turn(s, blocks):
             turned = psum.tile([P, 2, 2, P], F32, name="turned", tag="turned", bufs=4)
             for place, b in enumerate(blocks):
-                if b == 0 and s == 1:
-                    picked = first
-                else:
+                if (s, b) not in picked:
                     name = "picked%d_%d" % (s, b)
-                    picked = keep.tile([P, I], BF16, name=name, tag=after.get((s, b), name), align_bytes=64)
-                    window = stores[s][b][:]
-                    if (s, b) == (0, 1):
-                        nc.scalar.activation(picked[:, 0:256], window.indirect(store_lists[s][:, 0:16]), COPY)
-                        nc.vector.tensor_copy(picked[:, 256:512], window.indirect(store_lists[s][:, 16:32]))
-                    else:
-                        nc.scalar.activation(picked[:], window.indirect(store_lists[s][:]), COPY)
-                words = picked[:].bitcast(F32)
+                    picked[s, b] = keep.tile([P, I], BF16, name=name, tag=after.get((s, b), name), align_bytes=64)
+                    nc.scalar.activation(picked[s, b][:], stores[s][b][:].indirect(store_lists[s][:]), COPY)
+                words = picked[s, b][:].bitcast(F32)
                 for u in range(2):
                     nc.tensor.transpose(turned[:, place, u, :], words[:, u : 2 * P : 2], ident[:])
             return turned
 
-        def weave(leave, grouped, turned):
-            leave(
+        def weave(grouped, turned):
+            nc.scalar.copy(
                 grouped.rearrange("p w t -> p (w t)").bitcast(F32).rearrange("p (n e u) -> p n e u", n=2, u=2),
                 turned[:].rearrange("p n u e -> p n e u"),
             )
@@ -190,13 +184,6 @@ def tile_attend_tab_looked_twostores_kernel(
             sb("val_codes0", [P, E], U32),
             keep.tile([P, E], U32, name="val_codes1", tag="planes1", align_bytes=64),
         ]
-        val_bf1 = keep.tile([P, E, PACK], BF16, name="val_bf1", tag="val_bf1", align_bytes=64)
-        weave(nc.scalar.copy, val_bf1[:, 0:256, :], turn(1, (0, 1)))
-        weave(nc.scalar.copy, val_bf1[:, 256:512, :], turn(1, (2, 3)))
-        quantize(val_codes[1][:], val_scales[1][:], val_bf1[:])
-        table_bf[0] = keep.tile([P, J, PACK], BF16, name="table_bf0", tag="val_bf1", align_bytes=64)
-        dst, src = woven(table_bf[0][:], planes[0][:])
-        nc.vector.tensor_copy(dst, src)
         accs = [psum.tile([P, J], F32, name="acc%d" % b, tag="wide_bank", bufs=4) for b in range(4)]
 
         def product(s):
@@ -212,18 +199,24 @@ def tile_attend_tab_looked_twostores_kernel(
                     stop=(s == 0),
                 )
 
-        low = turn(0, (0, 1))
+        val_bf1 = keep.tile([P, E, PACK], BF16, name="val_bf1", tag="val_bf1", align_bytes=64)
+        weave(val_bf1[:, 0:256, :], turn(1, (0, 1)))
+        weave(val_bf1[:, 256:512, :], turn(1, (2, 3)))
+        quantize(val_codes[1][:], val_scales[1][:], val_bf1[:])
         product(1)
-        high = turn(0, (2, 3))
-        val_bf0a = sb("val_bf0a", [P, 256, PACK], BF16)
-        val_bf0b = sb("val_bf0b", [P, 256, PACK], BF16)
-        weave(nc.scalar.copy, val_bf0a[:], low)
-        weave(nc.scalar.copy, val_bf0b[:], high)
-        table_codes[0] = sb("table_codes0", [P, J], U32)
-        quantize(table_codes[0][:], table_scales[0][:], table_bf[0][:])
-        quantize(val_codes[0][:, 0:256], val_scales[0][:, 0:256], val_bf0a[:])
-        quantize(val_codes[0][:, 256:512], val_scales[0][:, 256:512], val_bf0b[:])
 
+        planes0 = keep.tile([P, PACK, J], BF16, name="planes0", tag="val_bf1", align_bytes=64)
+        for r in range(PACK):
+            scale_rows(planes0, 0, r)
+        nc.vector.tensor_copy(*woven(table_bf[0][:], planes0[:]))
+        quantize(table_codes[0][:], table_scales[0][:], table_bf[0][:])
+
+        low, high = turn(0, (0, 1)), turn(0, (2, 3))
+        val_bf0 = keep.tile([P, E, PACK], BF16, name="val_bf0", tag="last_store", align_bytes=64)
+        weave(val_bf0[:, 0:256, :], low)
+        weave(val_bf0[:, 256:512, :], high)
+        quantize(val_codes[0][:, 0:256], val_scales[0][:, 0:256], val_bf0[:, 0:256, :])
+        quantize(val_codes[0][:, 256:512], val_scales[0][:, 256:512], val_bf0[:, 256:512, :])
         product(0)
         for b in range(4):
             result = sb("result%d" % b, [P, J], F32)

from contextlib import ExitStack

import concourse.mybir as mybir
from concourse.masks import make_identity

F32 = mybir.dt.float32
BF16 = mybir.dt.bfloat16
I32 = mybir.dt.int32
U32 = mybir.dt.uint32
U16 = mybir.dt.uint16
U8 = mybir.dt.uint8
FP8X4 = mybir.dt.float8_e4m3fn_x4
ALU = mybir.AluOpType
COPY = mybir.ActivationFunctionType.Copy

P = 128
PACK = 4
D, T, I, J, U, E, Y = 512, 2048, 512, 512, 1024, 512, 1024
HALF = U // 2
FLOPS = 2 * D * I * U + 2 * 2 * I * E * J


def woven(dst, src):
    return (
        dst.rearrange("p (c i) t -> p c t i", i=4),
        src.rearrange("p t (c i) -> p c t i", i=4),
    )


def tile_attend_tab_looked_twostores_kernel(
    tc, keys_words, keys_scales, notes, rowf, rowf2, vals, vals2, offs, offs2, offs3, offs4, out
):
    nc = tc.nc
    with ExitStack() as ctx:
        keep = ctx.enter_context(tc.tile_pool(name="keep", bufs=1))
        psum = ctx.enter_context(tc.psum_pool(name="psum", bufs=1))

        def sb(name, shape, dtype):
            return keep.tile(shape, dtype, name=name, align_bytes=64)

        lists = {n: sb(n, [P, 32], U16) for n in ("offs", "offs2", "offs3", "offs4")}
        pool_words = sb("pool_words", [P, T], U32)
        pool_scales = sb("pool_scales", [P, T], U8)
        note_cols = [(0, 512), (512, 768), (768, 1024)]
        note_raw = [sb("note_raw%d" % n, [P, PACK, b - a], F32) for n, (a, b) in enumerate(note_cols)]
        factors = [sb("factor%d" % s, [P, PACK], F32) for s in range(2)]
        stores = [
            [sb("store0_%d" % b, [P, T], F32) for b in range(3)]
            + [keep.tile([P, T], F32, name="store0_3", tag="last_store", align_bytes=64)],
            [sb("store1_%d" % b, [P, Y], F32) for b in range(4)],
        ]
        notes_by_row = notes.rearrange("(p t) u -> p t u", t=PACK)

        nc.gpsimd.memset(pool_scales[:].bitcast(I32), 0)
        nc.sync.dma_start(lists["offs"][:], offs)
        nc.sync.dma_start(lists["offs3"][:], offs3)
        nc.sync.dma_start(lists["offs2"][:], offs2)
        nc.sync.dma_start(lists["offs4"][:], offs4)
        nc.sync.dma_start(out=note_raw[0][:], in_=notes_by_row[:, :, 0:512])
        for q in range(4):
            nc.sync.dma_start(
                out=pool_scales[32 * q : 32 * q + 4, :].bitcast(I32),
                in_=keys_scales[0, 4 * q : 4 * q + 4, :].bitcast(I32),
            )
        nc.sync.dma_start(
            out=pool_words[:].bitcast(I32),
            in_=keys_words[0].rearrange("p n t -> p (n t)").bitcast(I32),
        )
        for n in (1, 2):
            a, b = note_cols[n]
            nc.sync.dma_start(out=note_raw[n][:], in_=notes_by_row[:, :, a:b])
        for b in range(4):
            nc.sync.dma_start(out=stores[1][b][:], in_=vals2[b * P : (b + 1) * P, :])
        for s, src in enumerate((rowf, rowf2)):
            nc.sync.dma_start(out=factors[s][:], in_=src.rearrange("(p t) o -> p (t o)", t=PACK))
        for b in range(4):
            nc.sync.dma_start(out=stores[0][b][:], in_=vals[b * P : (b + 1) * P, :])

        ident = sb("ident", [P, P], F32)
        make_identity(nc, ident[:])

        key_scales = sb("key_scales", [P, I], U8)
        key_words = sb("key_words", [P, I], U32)
        nc.vector.tensor_copy(
            key_scales[:].rearrange("p (r s) -> p s r", r=PACK),
            pool_scales[:].indirect(lists["offs"][:]),
        )

        note_bf = [
            keep.tile([P, HALF, PACK], BF16, name="note_bf%d" % h, tag="note_bf%d" % h, align_bytes=64)
            for h in range(2)
        ]
        note_codes = [sb("note_codes%d" % h, [P, HALF], U32) for h in range(2)]
        note_scales = [sb("note_scales%d" % h, [P, HALF], U8) for h in range(2)]

        def quantize(codes, scales, grouped):
            nc.vector.quantize_mx(
                out=codes.bitcast(FP8X4), scales=scales, in_=grouped.rearrange("p w t -> p (w t)")
            )

        dst, src = woven(note_bf[0][:, 0:320, :], note_raw[0][:, :, 0:320])
        nc.vector.tensor_copy(dst, src)
        dst, src = woven(note_bf[0][:, 320:512, :], note_raw[0][:, :, 320:512])
        nc.scalar.activation(dst, src, COPY)
        quantize(note_codes[0][:], note_scales[0][:], note_bf[0][:])
        nc.vector.tensor_copy(
            key_words[:].rearrange("p (r s) -> p s r", r=PACK),
            pool_words[:].indirect(lists["offs"][:]),
        )
        for n in (1, 2):
            cols = slice((n - 1) * 256, n * 256)
            dst, src = woven(note_bf[1][:, cols, :], note_raw[n][:])
            nc.vector.tensor_copy(dst, src)
        for n in (1, 2):
            cols = slice((n - 1) * 256, n * 256)
            quantize(note_codes[1][:, cols], note_scales[1][:, cols], note_bf[1][:, cols, :])

        first = keep.tile([P, I], BF16, name="picked1_0", tag="note_bf1", align_bytes=64)
        nc.vector.tensor_copy(first[:], stores[1][0][:].indirect(lists["offs4"][:]))

        wide = [
            keep.tile([P, U], F32, name="wide%d" % r, tag="wide%d" % r, align_bytes=64) for r in range(PACK)
        ]
        for h in range(2):
            for r in range(PACK):
                bank = psum.tile([P, HALF], F32, name="wide_bank", tag="wide_bank", bufs=4)
                rows = slice(r * P, (r + 1) * P)
                nc.tensor.matmul_mx(
                    out=bank[:],
                    lhsT=key_words[:, rows].bitcast(FP8X4),
                    lhsT_scale=key_scales[:, rows],
                    rhs=note_codes[h][:].bitcast(FP8X4),
                    rhs_scale=note_scales[h][:],
                    start=True,
                    stop=True,
                )
                (nc.vector.tensor_copy if h == 1 and r > 0 else nc.scalar.copy)(wide[r][:, h * HALF : (h + 1) * HALF], bank[:])

        second = sb("picked1_1", [P, I], BF16)
        nc.vector.tensor_copy(second[:], stores[1][1][:].indirect(lists["offs4"][:]))
        picked = {(1, 0): first, (1, 1): second}

        def scale_rows(planes, s, r):
            nc.vector.tensor_scalar(planes[:, r, :], diffs[r][:], 0.0, factors[s][:, r : r + 1], ALU.max, ALU.mult)

        planes1 = keep.tile([P, PACK, J], BF16, name="planes1", tag="planes1", align_bytes=64)
        diffs = []
        for r in range(PACK):
            minus = sb("minus%d" % r, [P, J], F32)
            diffs.append(sb("diff%d" % r, [P, J], F32))
            nc.scalar.activation(minus[:], wide[r][:].indirect(lists["offs3"][:]), COPY)
            nc.vector.tensor_tensor(diffs[r][:], wide[r][:].indirect(lists["offs2"][:]), minus[:], ALU.subtract)
            scale_rows(planes1, 1, r)

        table_bf = [sb("table_bf%d" % s, [P, J, PACK], BF16) for s in range(2)]
        table_codes = [sb("table_codes%d" % s, [P, J], U32) for s in range(2)]
        table_scales = [sb("table_scales%d" % s, [P, J], U8) for s in range(2)]
        nc.vector.tensor_copy(*woven(table_bf[1][:], planes1[:]))
        quantize(table_codes[1][:], table_scales[1][:], table_bf[1][:])

        store_lists = (lists["offs"], lists["offs4"])
        after = {(1, 2): "wide0", (1, 3): "wide1", (0, 0): "wide2"}

        def turn(s, blocks):
            turned = psum.tile([P, 2, 2, P], F32, name="turned", tag="turned", bufs=4)
            for place, b in enumerate(blocks):
                if (s, b) not in picked:
                    name = "picked%d_%d" % (s, b)
                    picked[s, b] = keep.tile([P, I], BF16, name=name, tag=after.get((s, b), name), align_bytes=64)
                    nc.scalar.activation(picked[s, b][:], stores[s][b][:].indirect(store_lists[s][:]), COPY)
                words = picked[s, b][:].bitcast(F32)
                for u in range(2):
                    nc.tensor.transpose(turned[:, place, u, :], words[:, u : 2 * P : 2], ident[:])
            return turned

        def weave(grouped, turned):
            nc.scalar.copy(
                grouped.rearrange("p w t -> p (w t)").bitcast(F32).rearrange("p (n e u) -> p n e u", n=2, u=2),
                turned[:].rearrange("p n u e -> p n e u"),
            )

        val_scales = [sb("val_scales%d" % s, [P, E], U8) for s in range(2)]
        val_codes = [
            sb("val_codes0", [P, E], U32),
            keep.tile([P, E], U32, name="val_codes1", tag="planes1", align_bytes=64),
        ]
        accs = [psum.tile([P, J], F32, name="acc%d" % b, tag="wide_bank", bufs=4) for b in range(4)]

        def product(s):
            for b in range(4):
                cols = slice(b * P, (b + 1) * P)
                nc.tensor.matmul_mx(
                    out=accs[b][:],
                    lhsT=val_codes[s][:, cols].bitcast(FP8X4),
                    lhsT_scale=val_scales[s][:, cols],
                    rhs=table_codes[s][:].bitcast(FP8X4),
                    rhs_scale=table_scales[s][:],
                    start=(s == 1),
                    stop=(s == 0),
                )

        val_bf1 = keep.tile([P, E, PACK], BF16, name="val_bf1", tag="val_bf1", align_bytes=64)
        weave(val_bf1[:, 0:256, :], turn(1, (0, 1)))
        weave(val_bf1[:, 256:512, :], turn(1, (2, 3)))
        quantize(val_codes[1][:], val_scales[1][:], val_bf1[:])
        product(1)

        planes0 = keep.tile([P, PACK, J], BF16, name="planes0", tag="val_bf1", align_bytes=64)
        for r in range(PACK):
            scale_rows(planes0, 0, r)
        nc.vector.tensor_copy(*woven(table_bf[0][:], planes0[:]))
        quantize(table_codes[0][:], table_scales[0][:], table_bf[0][:])

        low, high = turn(0, (0, 1)), turn(0, (2, 3))
        val_bf0 = keep.tile([P, E, PACK], BF16, name="val_bf0", tag="last_store", align_bytes=64)
        weave(val_bf0[:, 0:256, :], low)
        weave(val_bf0[:, 256:512, :], high)
        quantize(val_codes[0][:, 0:256], val_scales[0][:, 0:256], val_bf0[:, 0:256, :])
        quantize(val_codes[0][:, 256:512], val_scales[0][:, 256:512], val_bf0[:, 256:512, :])
        product(0)
        for b in range(4):
            result = sb("result%d" % b, [P, J], F32)
            (nc.scalar.copy if b % 2 == 0 else nc.vector.tensor_copy)(result[:], accs[b][:])
            nc.sync.dma_start(out=out[b * P : (b + 1) * P, :], in_=result[:])
